import numpy as np
import ml_dtypes


def mxq(x, axis, fmt="e4m3"):
    dtype, down = {"e4m3": (ml_dtypes.float8_e4m3fn, 7), "e5m2": (ml_dtypes.float8_e5m2, 14)}[fmt]
    v = np.moveaxis(np.asarray(x, np.float32).astype(ml_dtypes.bfloat16).astype(np.float64), axis, -1)
    blocks = v.reshape(v.shape[:-1] + (-1, 32))
    amax = np.abs(blocks).max(-1, keepdims=True)
    byte = np.maximum(np.where(amax > 0, np.frexp(amax)[1] - 1 + 127, 0) - down, 1)
    scale = np.exp2(byte - 127.0)
    codes = (blocks / scale).astype(np.float32).astype(dtype).astype(np.float64)
    return np.moveaxis((codes * scale).reshape(v.shape), -1, axis)


WIDE = False


def mx_kscale(k):
    if not WIDE:
        return np.ones(k)
    levels = np.array([10, -10, 5, -5, 0])
    if k % 512:
        return np.exp2(np.random.permutation(np.resize(levels, k // 32))).repeat(32)
    a = np.empty((k // 512, 16))
    for p in range(k // 512):
        a[p, :8] = np.random.permutation(np.resize(levels, 8))
        for g in range(8):
            far = levels[np.abs(levels - a[p, g]) >= 10]
            a[p, g + 8] = far[np.random.randint(len(far))]
    return np.exp2(a.ravel()).repeat(32)


def f64(x):
    return np.asarray(x).astype(np.float64)


def split(x):
    m, e = np.frexp(f64(x))
    hi = np.ldexp(np.trunc(16.0 * m) / 16.0, e)
    return hi, f64(x) - hi


K, M, T = 1536, 1024, 1536


def setup_inputs():
    n = np.random.standard_normal
    s = mx_kscale(K)[:, None]
    return {
        "w": (n((K, M)) / np.sqrt(K) / s).astype(np.float32),
        "x": (n((K, T)) * s).astype(np.float32),
    }


def reference(w, x):
    w_hi, w_lo = split(w)
    w_hi_, w_lo_ = mxq(w_hi, 0, "e4m3"), mxq(w_lo, 0, "e4m3")
    x_ = mxq(f64(x), 0, "e4m3")
    y = w_hi_.T @ x_ + w_lo_.T @ x_
    return np.maximum(y, 0.0) ** 2

@@ -1,0 +1,179 @@
+from contextlib import ExitStack
+
+import concourse.mybir as mybir
+
+K, M, T = 1536, 1024, 1536
+FLOPS = 2 * 2 * K * M * T
+
+F32 = mybir.dt.float32
+BF16 = mybir.dt.bfloat16
+U32 = mybir.dt.uint32
+I32 = mybir.dt.int32
+U8 = mybir.dt.uint8
+FP8X4 = mybir.dt.float8_e4m3fn_x4
+ALU = mybir.AluOpType
+ACT = mybir.ActivationFunctionType
+
+P = 128
+PACK = 4
+K_PASS = P * PACK
+PASSES = K // K_PASS
+MT = 128
+NT = 512
+HI_MASK = 0xFFF0FFF0 - (1 << 32)
+LOADS = [
+    ("w", 0, 512, 0, "V"),
+    ("w", 0, 512, 1, "S"),
+    ("x", 0, 512, 0, 1),
+    ("w", 0, 512, 2, "S"),
+    ("x", 0, 512, 1, 1),
+    ("x", 0, 512, 2, 1),
+    ("x", 512, 512, 0, 0.5),
+    ("w", 512, 256, 0, "S"),
+    ("x", 512, 512, 1, 0.5),
+    ("w", 512, 256, 1, "S"),
+    ("x", 512, 512, 2, 0.5),
+    ("w", 512, 256, 2, "S"),
+    ("x", 1024, 512, 0, 0.5),
+    ("x", 1024, 512, 1, 0.5),
+    ("x", 1024, 512, 2, 0.5),
+    ("w", 768, 256, 0, "S"),
+    ("w", 768, 256, 1, "V"),
+    ("w", 768, 256, 2, "V"),
+]
+EPI = [["S","S"],["S","V"],["S","S"],["S","V"],["S","S"],["S","V"],["S","S"],["S","V"],["S","S"],["S","V"],["S","S"],["S","V"],["S","S"],["S","V"],["S","S"],["S","V"],["S","S"],["S","V"],["S","S"],["S","V"],["S","S"],["S","V"],["S","S"],["S","V"]]
+
+
+def tile_mix_hilo_fm_relu2_kernel(tc, w, x, out):
+    nc = tc.nc
+    with ExitStack() as ctx:
+        rawx = ctx.enter_context(tc.tile_pool(name="rawx", bufs=6))
+        raww = ctx.enter_context(tc.tile_pool(name="raww", bufs=3))
+        stage = ctx.enter_context(tc.tile_pool(name="stage", bufs=3))
+        keep = ctx.enter_context(tc.tile_pool(name="keep", bufs=1))
+        outs = ctx.enter_context(tc.tile_pool(name="outs", bufs=4))
+        psum = ctx.enter_context(tc.psum_pool(name="psum", bufs=8))
+
+        warm = keep.tile([P, 1], F32, name="warm")
+        nc.vector.memset(warm[:], 0.0)
+        nc.scalar.activation(out=warm[:], in_=warm[:], func=ACT.Square)
+
+        wq = {}
+        xq = {}
+
+        def load(src, pool, c0, width, k, name):
+            raw = pool.tile([P, PACK, width], F32, name=name)
+            rows = src[k * K_PASS : (k + 1) * K_PASS, c0 : c0 + width]
+            nc.sync.dma_start(out=raw[:], in_=rows.rearrange("(p j) c -> p j c", j=PACK))
+            return raw
+
+        def prep_w(c0, width, k, eng):
+            raw = load(w, raww, c0, width, k, "rw%d" % width)
+            both = stage.tile([P, 2, PACK * width], BF16, align_bytes=64, name="both%d" % width)
+            hi, lo = both[:, 0, :], both[:, 1, :]
+            words = raw[:].rearrange("p j c -> p (j c)").bitcast(BF16)
+            upper = words.rearrange("p (j c i h) -> p c j i h", j=PACK, i=4, h=2)[:, :, :, :, 1]
+            grouped = "p (c i j) -> p c j i"
+            hi_v = hi.rearrange(grouped, i=4, j=PACK)
+            lo_v = lo.rearrange(grouped, i=4, j=PACK)
+            if eng == "S":
+                nc.scalar.copy(out=hi_v, in_=upper)
+            else:
+                nc.vector.tensor_copy(out=hi_v, in_=upper)
+            nc.vector.tensor_scalar(
+                out=hi.bitcast(I32), in0=hi.bitcast(I32), scalar1=HI_MASK, scalar2=None, op0=ALU.bitwise_and
+            )
+            nc.vector.tensor_tensor(
+                out=lo_v, in0=raw[:].rearrange("p j (c i) -> p c j i", i=4), in1=hi_v, op=ALU.subtract
+            )
+            codes = keep.tile([P, 2 * width], U32, align_bytes=256, name="wc%d_%d" % (c0, k))
+            scales = keep.tile([P, 2 * width], U8, align_bytes=256, name="ws%d_%d" % (c0, k))
+            nc.vector.quantize_mx(
+                out=codes[:].bitcast(FP8X4), scales=scales[:], in_=both[:].rearrange("p h c -> p (h c)")
+            )
+            for m in range(c0, c0 + width, MT):
+                wq[m, k] = [
+                    (codes[:, a : a + MT].bitcast(FP8X4), scales[:, a : a + MT])
+                    for a in (m - c0, width + m - c0)
+                ]
+
+        def prep_x(c0, k, eng):
+            raw = load(x, rawx, c0, NT, k, "rx")
+            grp = stage.tile([P, PACK * NT], BF16, align_bytes=64, name="xg")
+            src = raw[:].rearrange("p j (c i) -> p j c i", i=4)
+            dst = grp[:].rearrange("p (c i j) -> p c j i", i=4, j=PACK)
+            cut = int(eng * NT) // 4
+            if cut > 0:
+                nc.scalar.copy(out=dst[:, :cut], in_=src[:, :, :cut].rearrange("p j c i -> p c j i"))
+            if cut < NT // 4:
+                nc.vector.tensor_copy(out=dst[:, cut:], in_=src[:, :, cut:].rearrange("p j c i -> p c j i"))
+            codes = keep.tile([P, NT], U32, align_bytes=256, name="xc%d_%d" % (c0, k))
+            scales = keep.tile([P, NT], U8, align_bytes=256, name="xs%d_%d" % (c0, k))
+            nc.vector.quantize_mx(out=codes[:].bitcast(FP8X4), scales=scales[:], in_=grp[:])
+            xq[c0, k] = (codes[:].bitcast(FP8X4), scales[:])
+
+        acc = {}
+        passed = {}
+        open_groups = []
+
+        def mm(m, t, k):
+            if (m, t) not in acc:
+                bank = psum.tile([MT, NT], F32, name="bank")
+                acc[m, t] = bank
+                passed[m, t] = 0
+            rhs, rhs_scale = xq[t, k]
+            for h in (0, 1):
+                lhsT, lhsT_scale = wq[m, k][h]
+                nc.tensor.matmul_mx(
+                    out=acc[m, t][:], lhsT=lhsT, lhsT_scale=lhsT_scale, rhs=rhs, rhs_scale=rhs_scale,
+                    start=(passed[m, t] == 0), stop=(passed[m, t] == 2 * PASSES - 1),
+                )
+                passed[m, t] += 1
+
+        count = [0]
+
+        def finish(m, t):
+            bank = acc[m, t]
+            r = outs.tile([MT, NT], F32, name="r")
+            o = outs.tile([MT, NT], F32, name="o")
+            e1, e2 = EPI[count[0]]
+            if e1 == "S":
+                nc.scalar.activation(out=r[:], in_=bank[:], func=ACT.Relu)
+            else:
+                nc.vector.tensor_scalar(out=r[:], in0=bank[:], scalar1=0.0, scalar2=None, op0=ALU.max)
+            if e2 == "S":
+                nc.scalar.activation(out=o[:], in_=r[:], func=ACT.Square)
+            else:
+                nc.vector.tensor_mul(o[:], r[:], r[:])
+            count[0] += 1
+            nc.sync.dma_start(out=out[m : m + MT, t : t + NT], in_=o[:])
+
+        done = set()
+        order = [(m, t) for m in range(0, M, MT) for t in range(0, T, NT)]
+        opened = []
+        for kind, c0, width, k, eng in LOADS:
+            if kind == "w":
+                prep_w(c0, width, k, eng)
+            else:
+                prep_x(c0, k, eng)
+            progress = True
+            while progress:
+                progress = False
+                ready = [
+                    (g not in opened, n, kk)
+                    for n, g in enumerate(order)
+                    for kk in range(PASSES)
+                    if (g, kk) not in done and (g[0], kk) in wq and (g[1], kk) in xq
+                    and (g in opened or len(opened) < 8)
+                ]
+                if ready:
+                    fresh, n, kk = min(ready)
+                    g = order[n]
+                    if fresh:
+                        opened.append(g)
+                    mm(g[0], g[1], kk)
+                    done.add((g, kk))
+                    progress = True
+                    if passed[g] == 2 * PASSES:
+                        opened.remove(g)
+                        finish(g[0], g[1])

@@ -20,160 +20,188 @@ K_PASS = P * PACK
 PASSES = K // K_PASS
 MT = 128
 NT = 512
+WU = 256
 HI_MASK = 0xFFF0FFF0 - (1 << 32)
+BANKS = 8
 LOADS = [
-    ("w", 0, 512, 0, "V"),
-    ("w", 0, 512, 1, "S"),
-    ("x", 0, 512, 0, 1),
-    ("w", 0, 512, 2, "S"),
-    ("x", 0, 512, 1, 1),
-    ("x", 0, 512, 2, 1),
-    ("x", 512, 512, 0, 0.5),
-    ("w", 512, 256, 0, "S"),
-    ("x", 512, 512, 1, 0.5),
-    ("w", 512, 256, 1, "S"),
-    ("x", 512, 512, 2, 0.5),
-    ("w", 512, 256, 2, "S"),
-    ("x", 1024, 512, 0, 0.5),
-    ("x", 1024, 512, 1, 0.5),
-    ("x", 1024, 512, 2, 0.5),
-    ("w", 768, 256, 0, "S"),
-    ("w", 768, 256, 1, "V"),
-    ("w", 768, 256, 2, "V"),
+    [("w", 0, 512), ("x", 0, 512)],
+    [("x", 512, 512)],
+    [("w", 512, 256)],
+    [("x", 1024, 512)],
+    [("w", 768, 256)],
 ]
-EPI = [["S","S"],["S","V"],["S","S"],["S","V"],["S","S"],["S","V"],["S","S"],["S","V"],["S","S"],["S","V"],["S","S"],["S","V"],["S","S"],["S","V"],["S","S"],["S","V"],["S","S"],["S","V"],["S","S"],["S","V"],["S","S"],["S","V"],["S","S"],["S","V"]]
+XSHARE = {0: 1.0, 512: 0.5, 1024: 1.0}
+VPACK = [(0, 0)]
+LEAD = 2
 
 
 def tile_mix_hilo_fm_relu2_kernel(tc, w, x, out):
     nc = tc.nc
     with ExitStack() as ctx:
-        rawx = ctx.enter_context(tc.tile_pool(name="rawx", bufs=6))
-        raww = ctx.enter_context(tc.tile_pool(name="raww", bufs=3))
+        raws = ctx.enter_context(tc.tile_pool(name="raws", bufs=1))
         stage = ctx.enter_context(tc.tile_pool(name="stage", bufs=3))
         keep = ctx.enter_context(tc.tile_pool(name="keep", bufs=1))
-        outs = ctx.enter_context(tc.tile_pool(name="outs", bufs=4))
-        psum = ctx.enter_context(tc.psum_pool(name="psum", bufs=8))
+        outs = ctx.enter_context(tc.tile_pool(name="outs", bufs=5))
+        psum = ctx.enter_context(tc.psum_pool(name="psum", bufs=BANKS))
+        ctx.enter_context(tc.manual_schedule())
 
         warm = keep.tile([P, 1], F32, name="warm")
         nc.vector.memset(warm[:], 0.0)
         nc.scalar.activation(out=warm[:], in_=warm[:], func=ACT.Square)
 
+        raw_of = {}
+        units = []
+        for kind, c0, width, k in [(a, b, c, d) for step in LOADS for d in range(PASSES) for a, b, c in step]:
+            raw = raws.tile([P, PACK, width], F32, name="raw_%s%d_%d" % (kind, c0, k))
+            src = (w if kind == "w" else x)[k * K_PASS : (k + 1) * K_PASS, c0 : c0 + width]
+            nc.sync.dma_start(out=raw[:], in_=src.rearrange("(p j) c -> p j c", j=PACK))
+            size = WU if kind == "w" else NT
+            for a in range(0, width, size):
+                units.append((kind, c0 + a, k))
+                raw_of[kind, c0 + a, k] = raw[:, :, a : a + size]
+
+        grouped = {}
         wq = {}
         xq = {}
+        GR = "p (c i j) -> p c j i"
 
-        def load(src, pool, c0, width, k, name):
-            raw = pool.tile([P, PACK, width], F32, name=name)
-            rows = src[k * K_PASS : (k + 1) * K_PASS, c0 : c0 + width]
-            nc.sync.dma_start(out=raw[:], in_=rows.rearrange("(p j) c -> p j c", j=PACK))
-            return raw
-
-        def prep_w(c0, width, k, eng):
-            raw = load(w, raww, c0, width, k, "rw%d" % width)
-            both = stage.tile([P, 2, PACK * width], BF16, align_bytes=64, name="both%d" % width)
-            hi, lo = both[:, 0, :], both[:, 1, :]
-            words = raw[:].rearrange("p j c -> p (j c)").bitcast(BF16)
-            upper = words.rearrange("p (j c i h) -> p c j i h", j=PACK, i=4, h=2)[:, :, :, :, 1]
-            grouped = "p (c i j) -> p c j i"
-            hi_v = hi.rearrange(grouped, i=4, j=PACK)
-            lo_v = lo.rearrange(grouped, i=4, j=PACK)
-            if eng == "S":
-                nc.scalar.copy(out=hi_v, in_=upper)
-            else:
-                nc.vector.tensor_copy(out=hi_v, in_=upper)
-            nc.vector.tensor_scalar(
-                out=hi.bitcast(I32), in0=hi.bitcast(I32), scalar1=HI_MASK, scalar2=None, op0=ALU.bitwise_and
-            )
-            nc.vector.tensor_tensor(
-                out=lo_v, in0=raw[:].rearrange("p j (c i) -> p c j i", i=4), in1=hi_v, op=ALU.subtract
-            )
-            codes = keep.tile([P, 2 * width], U32, align_bytes=256, name="wc%d_%d" % (c0, k))
-            scales = keep.tile([P, 2 * width], U8, align_bytes=256, name="ws%d_%d" % (c0, k))
-            nc.vector.quantize_mx(
-                out=codes[:].bitcast(FP8X4), scales=scales[:], in_=both[:].rearrange("p h c -> p (h c)")
-            )
-            for m in range(c0, c0 + width, MT):
-                wq[m, k] = [
-                    (codes[:, a : a + MT].bitcast(FP8X4), scales[:, a : a + MT])
-                    for a in (m - c0, width + m - c0)
-                ]
-
-        def prep_x(c0, k, eng):
-            raw = load(x, rawx, c0, NT, k, "rx")
-            grp = stage.tile([P, PACK * NT], BF16, align_bytes=64, name="xg")
-            src = raw[:].rearrange("p j (c i) -> p j c i", i=4)
-            dst = grp[:].rearrange("p (c i j) -> p c j i", i=4, j=PACK)
-            cut = int(eng * NT) // 4
-            if cut > 0:
-                nc.scalar.copy(out=dst[:, :cut], in_=src[:, :, :cut].rearrange("p j c i -> p c j i"))
-            if cut < NT // 4:
-                nc.vector.tensor_copy(out=dst[:, cut:], in_=src[:, :, cut:].rearrange("p j c i -> p c j i"))
-            codes = keep.tile([P, NT], U32, align_bytes=256, name="xc%d_%d" % (c0, k))
-            scales = keep.tile([P, NT], U8, align_bytes=256, name="xs%d_%d" % (c0, k))
-            nc.vector.quantize_mx(out=codes[:].bitcast(FP8X4), scales=scales[:], in_=grp[:])
-            xq[c0, k] = (codes[:].bitcast(FP8X4), scales[:])
-
-        acc = {}
-        passed = {}
-        open_groups = []
-
-        def mm(m, t, k):
-            if (m, t) not in acc:
-                bank = psum.tile([MT, NT], F32, name="bank")
-                acc[m, t] = bank
-                passed[m, t] = 0
-            rhs, rhs_scale = xq[t, k]
-            for h in (0, 1):
-                lhsT, lhsT_scale = wq[m, k][h]
-                nc.tensor.matmul_mx(
-                    out=acc[m, t][:], lhsT=lhsT, lhsT_scale=lhsT_scale, rhs=rhs, rhs_scale=rhs_scale,
-                    start=(passed[m, t] == 0), stop=(passed[m, t] == 2 * PASSES - 1),
-                )
-                passed[m, t] += 1
-
-        count = [0]
-
-        def finish(m, t):
-            bank = acc[m, t]
-            r = outs.tile([MT, NT], F32, name="r")
-            o = outs.tile([MT, NT], F32, name="o")
-            e1, e2 = EPI[count[0]]
-            if e1 == "S":
-                nc.scalar.activation(out=r[:], in_=bank[:], func=ACT.Relu)
-            else:
-                nc.vector.tensor_scalar(out=r[:], in0=bank[:], scalar1=0.0, scalar2=None, op0=ALU.max)
-            if e2 == "S":
-                nc.scalar.activation(out=o[:], in_=r[:], func=ACT.Square)
-            else:
-                nc.vector.tensor_mul(o[:], r[:], r[:])
-            count[0] += 1
-            nc.sync.dma_start(out=out[m : m + MT, t : t + NT], in_=o[:])
-
-        done = set()
-        order = [(m, t) for m in range(0, M, MT) for t in range(0, T, NT)]
-        opened = []
-        for kind, c0, width, k, eng in LOADS:
+        def first(u):
+            kind, c0, k = u
+            raw = raw_of[u]
             if kind == "w":
-                prep_w(c0, width, k, eng)
+                both = stage.tile([P, 2, PACK * WU], BF16, align_bytes=64, name="both")
+                grouped[u] = both
+                upper = raw.bitcast(BF16).rearrange("p j (c i h) -> p c j i h", i=4, h=2)[:, :, :, :, 1]
+                dst = both[:, 0, :].rearrange(GR, i=4, j=PACK)
+                if (c0, k) in VPACK:
+                    nc.vector.tensor_copy(out=dst, in_=upper)
+                else:
+                    nc.scalar.copy(out=dst, in_=upper)
             else:
-                prep_x(c0, k, eng)
-            progress = True
-            while progress:
-                progress = False
+                grp = stage.tile([P, PACK * NT], BF16, align_bytes=64, name="grp")
+                grouped[u] = grp
+                cut = int(XSHARE[c0] * NT) // 4
+                src = raw.rearrange("p j (c i) -> p c j i", i=4)
+                dst = grp[:].rearrange(GR, i=4, j=PACK)
+                nc.scalar.copy(out=dst[:, :cut], in_=src[:, :cut])
+
+        def second(u):
+            kind, c0, k = u
+            raw = raw_of[u]
+            if kind == "w":
+                hi = grouped[u][:, 0, :].bitcast(I32)
+                nc.vector.tensor_scalar(out=hi, in0=hi, scalar1=HI_MASK, scalar2=None, op0=ALU.bitwise_and)
+            else:
+                cut = int(XSHARE[c0] * NT) // 4
+                if cut < NT // 4:
+                    src = raw.rearrange("p j (c i) -> p c j i", i=4)
+                    dst = grouped[u][:].rearrange(GR, i=4, j=PACK)
+                    nc.vector.tensor_copy(out=dst[:, cut:], in_=src[:, cut:])
+
+        def subtract(u):
+            if u[0] == "w":
+                both = grouped[u]
+                nc.vector.tensor_tensor(
+                    out=both[:, 1, :].rearrange(GR, i=4, j=PACK),
+                    in0=raw_of[u].rearrange("p j (c i) -> p c j i", i=4),
+                    in1=both[:, 0, :].rearrange(GR, i=4, j=PACK),
+                    op=ALU.subtract,
+                )
+
+        def quantize(u):
+            kind, c0, k = u
+            width = 2 * WU if kind == "w" else NT
+            codes = keep.tile([P, width], U32, align_bytes=256, name="codes_%s%d_%d" % u)
+            scales = keep.tile([P, width], U8, align_bytes=256, name="scales_%s%d_%d" % u)
+            src = grouped.pop(u)
+            nc.vector.quantize_mx(
+                out=codes[:].bitcast(FP8X4),
+                scales=scales[:],
+                in_=src[:].rearrange("p h c -> p (h c)") if kind == "w" else src[:],
+            )
+            if kind == "w":
+                for a in range(0, WU, MT):
+                    wq[c0 + a, k] = [
+                        (codes[:, b : b + MT].bitcast(FP8X4), scales[:, b : b + MT]) for b in (a, WU + a)
+                    ]
+            else:
+                xq[c0, k] = (codes[:].bitcast(FP8X4), scales[:])
+
+        groups = [(m, t) for m in range(0, M, MT) for t in range(0, T, NT)]
+        acc = {}
+        todo = {g: list(range(PASSES)) for g in groups}
+        full = []
+        squares = []
+        state = {"free": BANKS, "n": 0}
+
+        def multiply():
+            while True:
                 ready = [
-                    (g not in opened, n, kk)
-                    for n, g in enumerate(order)
-                    for kk in range(PASSES)
-                    if (g, kk) not in done and (g[0], kk) in wq and (g[1], kk) in xq
-                    and (g in opened or len(opened) < 8)
+                    (g not in acc, n, k)
+                    for n, g in enumerate(groups)
+                    for k in todo[g]
+                    if (g[0], k) in wq and (g[1], k) in xq and (g in acc or state["free"] > 0)
                 ]
-                if ready:
-                    fresh, n, kk = min(ready)
-                    g = order[n]
-                    if fresh:
-                        opened.append(g)
-                    mm(g[0], g[1], kk)
-                    done.add((g, kk))
-                    progress = True
-                    if passed[g] == 2 * PASSES:
-                        opened.remove(g)
-                        finish(g[0], g[1])
+                if not ready:
+                    return
+                fresh, n, k = min(ready)
+                m, t = groups[n]
+                if fresh:
+                    bank = psum.tile([MT, NT], F32, name="bank")
+                    acc[m, t] = bank
+                    state["free"] -= 1
+                rhs, rhs_scale = xq[t, k]
+                first_pass = len(todo[m, t]) == PASSES
+                todo[m, t].remove(k)
+                last_pass = not todo[m, t]
+                for h, (lhsT, lhsT_scale) in enumerate(wq[m, k]):
+                    nc.tensor.matmul_mx(
+                        out=acc[m, t][:], lhsT=lhsT, lhsT_scale=lhsT_scale, rhs=rhs, rhs_scale=rhs_scale,
+                        start=first_pass and h == 0, stop=last_pass and h == 1,
+                    )
+                if last_pass:
+                    full.append((m, t))
+
+        EPI = ["VS","VS","VS","VS","VS","VS","VS","VS","VS","VS","VS","VS","VS","VS","VS","VS","VS","VS","VS","VS","VS","VS","VS","VS"]
+
+        def relu(count):
+            for g in full[:count]:
+                r = outs.tile([MT, NT], F32, name="r")
+                e = EPI[state["n"]]
+                state["n"] += 1
+                if e[0] == "V":
+                    nc.vector.tensor_scalar(out=r[:], in0=acc[g][:], scalar1=0.0, scalar2=None, op0=ALU.max)
+                else:
+                    nc.scalar.activation(out=r[:], in_=acc[g][:], func=ACT.Relu)
+                state["free"] += 1
+                squares.append((g, r, e[1]))
+            del_n = min(count, len(full))
+            full[:] = full[del_n:]
+
+        def square():
+            while squares:
+                (m, t), r, e = squares.pop(0)
+                o = outs.tile([MT, NT], F32, name="o")
+                if e == "V":
+                    nc.vector.tensor_mul(o[:], r[:], r[:])
+                else:
+                    nc.scalar.activation(out=o[:], in_=r[:], func=ACT.Square)
+                nc.sync.dma_start(out=out[m : m + MT, t : t + NT], in_=o[:])
+
+        n = len(units)
+        for s in range(-LEAD, n + 2):
+            if 0 <= s + LEAD < n:
+                first(units[s + LEAD])
+            if 0 <= s + 1 < n:
+                second(units[s + 1])
+            if 0 <= s - 1 < n:
+                quantize(units[s - 1])
+            square()
+            if 0 <= s < n:
+                subtract(units[s])
+            multiply()
+            relu(1 if s <= n else 2)
+        while full or squares:
+            square()
+            relu(2)
+            multiply()

@@ -23,25 +23,214 @@ NT = 512
 WU = 256
 HI_MASK = 0xFFF0FFF0 - (1 << 32)
 BANKS = 8
-LOADS = [
-    [("w", 0, 512), ("x", 0, 512)],
-    [("x", 512, 512)],
-    [("w", 512, 256)],
-    [("x", 1024, 512)],
-    [("w", 768, 256)],
+LOADS = [["w",0,512,0],["x",0,512,0],["w",0,512,1],["x",0,512,1],["w",0,512,2],["x",0,512,2],["x",512,512,0],["x",512,512,1],["x",512,512,2],["w",512,256,0],["w",512,256,1],["w",512,256,2],["x",1024,512,0],["x",1024,512,1],["x",1024,512,2],["w",768,256,0],["w",768,256,1],["w",768,256,2]]
+XSHARE = {(512, 2): 0.25, (0, 1): 1, (1024, 0): 0.75, (1024, 2): 1, (512, 1): 0.25, (512, 0): 1, (1024, 1): 0.5, (0, 2): 1, (0, 0): 1}
+OPS = [
+    ["pack",256,0,0,"S"],
+    ["pack",0,0,0,"V"],
+    ["mask",0,0,0,"V"],
+    ["mask",256,0,0,"V"],
+    ["sub",0,0,0,"V"],
+    ["castS",0,0,0,"S"],
+    ["sub",256,0,0,"V"],
+    ["qw",0,0,0,"V"],
+    ["qw",256,0,0,"V"],
+    ["pack",256,1,0,"S"],
+    ["qx",0,0,0,"V"],
+    ["pack",0,1,0,"V"],
+    ["mm",0,0,0,"P"],
+    ["mm",128,0,0,"P"],
+    ["mask",256,1,0,"V"],
+    ["mask",0,1,0,"V"],
+    ["mm",256,0,0,"P"],
+    ["sub",256,1,0,"V"],
+    ["castS",0,1,0,"S"],
+    ["mm",384,0,0,"P"],
+    ["sub",0,1,0,"V"],
+    ["qw",256,1,0,"V"],
+    ["pack",0,2,0,"S"],
+    ["qw",0,1,0,"V"],
+    ["qx",0,1,0,"V"],
+    ["pack",256,2,0,"S"],
+    ["mask",0,2,0,"V"],
+    ["mm",0,0,1,"P"],
+    ["sub",0,2,0,"V"],
+    ["mm",128,0,1,"P"],
+    ["castS",0,2,0,"S"],
+    ["mm",256,0,1,"P"],
+    ["mask",256,2,0,"V"],
+    ["mm",384,0,1,"P"],
+    ["qw",0,2,0,"V"],
+    ["sub",256,2,0,"V"],
+    ["castS",512,0,0,"S"],
+    ["qx",0,2,0,"V"],
+    ["qw",256,2,0,"V"],
+    ["mm",0,0,2,"P"],
+    ["mm",128,0,2,"P"],
+    ["relu",0,0,0,"V"],
+    ["mm",256,0,2,"P"],
+    ["relu",128,0,0,"V"],
+    ["sq",0,0,0,"S"],
+    ["mm",384,0,2,"P"],
+    ["qx",512,0,0,"V"],
+    ["castS",512,1,0,"S"],
+    ["castV",512,1,0,"V"],
+    ["mm",0,512,0,"P"],
+    ["sq",128,0,0,"S"],
+    ["mm",128,512,0,"P"],
+    ["relu",256,0,0,"S"],
+    ["mm",256,512,0,"P"],
+    ["qx",512,1,0,"V"],
+    ["relu",384,0,0,"S"],
+    ["mm",384,512,0,"P"],
+    ["castV",512,2,0,"V"],
+    ["castS",512,2,0,"S"],
+    ["mm",0,512,1,"P"],
+    ["sq",256,0,0,"V"],
+    ["mm",128,512,1,"P"],
+    ["pack",512,0,0,"S"],
+    ["qx",512,2,0,"V"],
+    ["mm",256,512,1,"P"],
+    ["sq",384,0,0,"V"],
+    ["mm",384,512,1,"P"],
+    ["pack",512,1,0,"S"],
+    ["mask",512,0,0,"V"],
+    ["mm",0,512,2,"P"],
+    ["sub",512,0,0,"V"],
+    ["mm",128,512,2,"P"],
+    ["mm",256,512,2,"P"],
+    ["pack",512,2,0,"S"],
+    ["mm",384,512,2,"P"],
+    ["mask",512,1,0,"V"],
+    ["qw",512,0,0,"V"],
+    ["relu",384,512,0,"S"],
+    ["sub",512,1,0,"V"],
+    ["mm",512,0,0,"P"],
+    ["mm",512,512,0,"P"],
+    ["mask",512,2,0,"V"],
+    ["castS",1024,0,0,"S"],
+    ["mm",640,0,0,"P"],
+    ["qw",512,1,0,"V"],
+    ["mm",640,512,0,"P"],
+    ["sub",512,2,0,"V"],
+    ["mm",512,0,1,"P"],
+    ["mm",512,512,1,"P"],
+    ["castV",1024,0,0,"V"],
+    ["mm",640,0,1,"P"],
+    ["qw",512,2,0,"V"],
+    ["castS",1024,1,0,"S"],
+    ["mm",640,512,1,"P"],
+    ["qx",1024,0,0,"V"],
+    ["mm",512,0,2,"P"],
+    ["castV",1024,1,0,"V"],
+    ["mm",512,512,2,"P"],
+    ["relu",512,0,0,"S"],
+    ["relu",0,512,0,"V"],
+    ["mm",640,0,2,"P"],
+    ["relu",512,512,0,"S"],
+    ["qx",1024,1,0,"V"],
+    ["mm",640,512,2,"P"],
+    ["castS",1024,2,0,"S"],
+    ["relu",128,512,0,"V"],
+    ["mm",0,1024,0,"P"],
+    ["relu",256,512,0,"V"],
+    ["mm",0,1024,1,"P"],
+    ["pack",768,0,0,"V"],
+    ["mm",128,1024,0,"P"],
+    ["sq",384,512,0,"V"],
+    ["mm",128,1024,1,"P"],
+    ["sq",0,512,0,"S"],
+    ["qx",1024,2,0,"V"],
+    ["mm",256,1024,0,"P"],
+    ["sq",128,512,0,"S"],
+    ["mm",256,1024,1,"P"],
+    ["mask",768,0,0,"V"],
+    ["sq",256,512,0,"S"],
+    ["pack",768,1,0,"V"],
+    ["mm",0,1024,2,"P"],
+    ["sq",512,512,0,"S"],
+    ["sub",768,0,0,"V"],
+    ["mm",128,1024,2,"P"],
+    ["relu",640,512,0,"S"],
+    ["mm",256,1024,2,"P"],
+    ["relu",128,1024,0,"S"],
+    ["mask",768,1,0,"V"],
+    ["mm",384,1024,0,"P"],
+    ["qw",768,0,0,"V"],
+    ["sq",128,1024,0,"S"],
+    ["mm",384,1024,1,"P"],
+    ["sub",768,1,0,"V"],
+    ["mm",384,1024,2,"P"],
+    ["mm",512,1024,0,"P"],
+    ["pack",768,2,0,"V"],
+    ["mm",512,1024,1,"P"],
+    ["qw",768,1,0,"V"],
+    ["mm",512,1024,2,"P"],
+    ["mask",768,2,0,"V"],
+    ["mm",640,1024,0,"P"],
+    ["sq",512,0,0,"V"],
+    ["mm",640,1024,1,"P"],
+    ["sub",768,2,0,"V"],
+    ["mm",640,1024,2,"P"],
+    ["mm",768,0,0,"P"],
+    ["relu",640,0,0,"V"],
+    ["mm",768,0,1,"P"],
+    ["qw",768,2,0,"V"],
+    ["sq",640,0,0,"S"],
+    ["mm",768,512,0,"P"],
+    ["sq",640,512,0,"V"],
+    ["mm",768,0,2,"P"],
+    ["relu",0,1024,0,"V"],
+    ["mm",768,512,1,"P"],
+    ["relu",768,0,0,"S"],
+    ["relu",256,1024,0,"V"],
+    ["mm",768,512,2,"P"],
+    ["sq",0,1024,0,"S"],
+    ["relu",384,1024,0,"V"],
+    ["mm",768,1024,0,"P"],
+    ["sq",256,1024,0,"S"],
+    ["relu",512,1024,0,"V"],
+    ["mm",768,1024,1,"P"],
+    ["sq",384,1024,0,"V"],
+    ["mm",768,1024,2,"P"],
+    ["sq",512,1024,0,"V"],
+    ["mm",896,0,0,"P"],
+    ["relu",640,1024,0,"V"],
+    ["mm",896,0,1,"P"],
+    ["sq",768,0,0,"V"],
+    ["mm",896,0,2,"P"],
+    ["sq",640,1024,0,"S"],
+    ["relu",768,512,0,"V"],
+    ["mm",896,512,0,"P"],
+    ["relu",768,1024,0,"V"],
+    ["mm",896,512,1,"P"],
+    ["sq",768,512,0,"S"],
+    ["relu",896,0,0,"V"],
+    ["mm",896,512,2,"P"],
+    ["sq",768,1024,0,"S"],
+    ["sq",896,0,0,"S"],
+    ["relu",896,512,0,"V"],
+    ["sq",896,512,0,"S"],
+    ["mmh",896,1024,0,0],
+    ["mmh",896,1024,1,0],
+    ["mmh",896,1024,2,0],
+    ["mmh",896,1024,0,1],
+    ["mmh",896,1024,1,1],
+    ["mmh",896,1024,2,1],
+    ["reluh",896,1024,0,"V"],
+    ["sqh",896,1024,0,"S"],
+    ["reluh",896,1024,1,"V"],
+    ["sqh",896,1024,1,"S"],
 ]
-XSHARE = {0: 1.0, 512: 0.5, 1024: 1.0}
-VPACK = [(0, 0)]
-LEAD = 2
 
 
 def tile_mix_hilo_fm_relu2_kernel(tc, w, x, out):
     nc = tc.nc
     with ExitStack() as ctx:
         raws = ctx.enter_context(tc.tile_pool(name="raws", bufs=1))
-        stage = ctx.enter_context(tc.tile_pool(name="stage", bufs=3))
+        stage = ctx.enter_context(tc.tile_pool(name="stage", bufs=4))
         keep = ctx.enter_context(tc.tile_pool(name="keep", bufs=1))
-        outs = ctx.enter_context(tc.tile_pool(name="outs", bufs=5))
+        outs = ctx.enter_context(tc.tile_pool(name="outs", bufs=12))
         psum = ctx.enter_context(tc.psum_pool(name="psum", bufs=BANKS))
         ctx.enter_context(tc.manual_schedule())
 
@@ -50,63 +239,57 @@ def tile_mix_hilo_fm_relu2_kernel(tc, w, x, out):
         nc.scalar.activation(out=warm[:], in_=warm[:], func=ACT.Square)
 
         raw_of = {}
-        units = []
-        for kind, c0, width, k in [(a, b, c, d) for step in LOADS for d in range(PASSES) for a, b, c in step]:
+        for kind, c0, width, k in LOADS:
             raw = raws.tile([P, PACK, width], F32, name="raw_%s%d_%d" % (kind, c0, k))
             src = (w if kind == "w" else x)[k * K_PASS : (k + 1) * K_PASS, c0 : c0 + width]
             nc.sync.dma_start(out=raw[:], in_=src.rearrange("(p j) c -> p j c", j=PACK))
             size = WU if kind == "w" else NT
             for a in range(0, width, size):
-                units.append((kind, c0 + a, k))
                 raw_of[kind, c0 + a, k] = raw[:, :, a : a + size]
 
         grouped = {}
         wq = {}
         xq = {}
+        acc = {}
+        relus = {}
+        passes = {}
         GR = "p (c i j) -> p c j i"
 
-        def first(u):
-            kind, c0, k = u
-            raw = raw_of[u]
-            if kind == "w":
-                both = stage.tile([P, 2, PACK * WU], BF16, align_bytes=64, name="both")
-                grouped[u] = both
-                upper = raw.bitcast(BF16).rearrange("p j (c i h) -> p c j i h", i=4, h=2)[:, :, :, :, 1]
-                dst = both[:, 0, :].rearrange(GR, i=4, j=PACK)
-                if (c0, k) in VPACK:
-                    nc.vector.tensor_copy(out=dst, in_=upper)
-                else:
-                    nc.scalar.copy(out=dst, in_=upper)
+        def pack(c0, k, e):
+            both = stage.tile([P, 2, PACK * WU], BF16, align_bytes=64, name="both")
+            grouped["w", c0, k] = both
+            upper = raw_of["w", c0, k].bitcast(BF16).rearrange("p j (c i h) -> p c j i h", i=4, h=2)[:, :, :, :, 1]
+            dst = both[:, 0, :].rearrange(GR, i=4, j=PACK)
+            if e == "V":
+                nc.vector.tensor_copy(out=dst, in_=upper)
             else:
+                nc.scalar.copy(out=dst, in_=upper)
+
+        def cast(c0, k, e):
+            u = ("x", c0, k)
+            if u not in grouped:
                 grp = stage.tile([P, PACK * NT], BF16, align_bytes=64, name="grp")
                 grouped[u] = grp
-                cut = int(XSHARE[c0] * NT) // 4
-                src = raw.rearrange("p j (c i) -> p c j i", i=4)
-                dst = grp[:].rearrange(GR, i=4, j=PACK)
+            cut = int(XSHARE.get((c0, k), 1.0) * NT) // 4
+            src = raw_of[u].rearrange("p j (c i) -> p c j i", i=4)
+            dst = grouped[u][:].rearrange(GR, i=4, j=PACK)
+            if e == "S":
                 nc.scalar.copy(out=dst[:, :cut], in_=src[:, :cut])
-
-        def second(u):
-            kind, c0, k = u
-            raw = raw_of[u]
-            if kind == "w":
-                hi = grouped[u][:, 0, :].bitcast(I32)
-                nc.vector.tensor_scalar(out=hi, in0=hi, scalar1=HI_MASK, scalar2=None, op0=ALU.bitwise_and)
             else:
-                cut = int(XSHARE[c0] * NT) // 4
-                if cut < NT // 4:
-                    src = raw.rearrange("p j (c i) -> p c j i", i=4)
-                    dst = grouped[u][:].rearrange(GR, i=4, j=PACK)
-                    nc.vector.tensor_copy(out=dst[:, cut:], in_=src[:, cut:])
+                nc.vector.tensor_copy(out=dst[:, cut:], in_=src[:, cut:])
 
-        def subtract(u):
-            if u[0] == "w":
-                both = grouped[u]
-                nc.vector.tensor_tensor(
-                    out=both[:, 1, :].rearrange(GR, i=4, j=PACK),
-                    in0=raw_of[u].rearrange("p j (c i) -> p c j i", i=4),
-                    in1=both[:, 0, :].rearrange(GR, i=4, j=PACK),
-                    op=ALU.subtract,
-                )
+        def mask(c0, k):
+            hi = grouped["w", c0, k][:, 0, :].bitcast(I32)
+            nc.vector.tensor_scalar(out=hi, in0=hi, scalar1=HI_MASK, scalar2=None, op0=ALU.bitwise_and)
+
+        def subtract(c0, k):
+            both = grouped["w", c0, k]
+            nc.vector.tensor_tensor(
+                out=both[:, 1, :].rearrange(GR, i=4, j=PACK),
+                in0=raw_of["w", c0, k].rearrange("p j (c i) -> p c j i", i=4),
+                in1=both[:, 0, :].rearrange(GR, i=4, j=PACK),
+                op=ALU.subtract,
+            )
 
         def quantize(u):
             kind, c0, k = u
@@ -127,81 +310,81 @@ def tile_mix_hilo_fm_relu2_kernel(tc, w, x, out):
             else:
                 xq[c0, k] = (codes[:].bitcast(FP8X4), scales[:])
 
-        groups = [(m, t) for m in range(0, M, MT) for t in range(0, T, NT)]
-        acc = {}
-        todo = {g: list(range(PASSES)) for g in groups}
-        full = []
-        squares = []
-        state = {"free": BANKS, "n": 0}
+        def multiply(m, t, k):
+            n = passes.get((m, t), 0)
+            if n == 0:
+                bank = psum.tile([MT, NT], F32, name="bank")
+                acc[m, t] = bank
+            rhs, rhs_scale = xq[t, k]
+            for h, (lhsT, lhsT_scale) in enumerate(wq[m, k]):
+                nc.tensor.matmul_mx(
+                    out=acc[m, t][:], lhsT=lhsT, lhsT_scale=lhsT_scale, rhs=rhs, rhs_scale=rhs_scale,
+                    start=n == 0 and h == 0, stop=n == PASSES - 1 and h == 1,
+                )
+            passes[m, t] = n + 1
 
-        def multiply():
-            while True:
-                ready = [
-                    (g not in acc, n, k)
-                    for n, g in enumerate(groups)
-                    for k in todo[g]
-                    if (g[0], k) in wq and (g[1], k) in xq and (g in acc or state["free"] > 0)
-                ]
-                if not ready:
-                    return
-                fresh, n, k = min(ready)
-                m, t = groups[n]
-                if fresh:
-                    bank = psum.tile([MT, NT], F32, name="bank")
-                    acc[m, t] = bank
-                    state["free"] -= 1
-                rhs, rhs_scale = xq[t, k]
-                first_pass = len(todo[m, t]) == PASSES
-                todo[m, t].remove(k)
-                last_pass = not todo[m, t]
-                for h, (lhsT, lhsT_scale) in enumerate(wq[m, k]):
-                    nc.tensor.matmul_mx(
-                        out=acc[m, t][:], lhsT=lhsT, lhsT_scale=lhsT_scale, rhs=rhs, rhs_scale=rhs_scale,
-                        start=first_pass and h == 0, stop=last_pass and h == 1,
-                    )
-                if last_pass:
-                    full.append((m, t))
+        def relu(m, t, e):
+            r = outs.tile([MT, NT], F32, name="r")
+            relus[m, t] = r
+            if e == "V":
+                nc.vector.tensor_scalar(out=r[:], in0=acc[m, t][:], scalar1=0.0, scalar2=None, op0=ALU.max)
+            else:
+                nc.scalar.activation(out=r[:], in_=acc[m, t][:], func=ACT.Relu)
 
-        EPI = ["VS","VS","VS","VS","VS","VS","VS","VS","VS","VS","VS","VS","VS","VS","VS","VS","VS","VS","VS","VS","VS","VS","VS","VS"]
+        def square(m, t, e):
+            r = relus[m, t]
+            if e == "V":
+                nc.vector.tensor_mul(r[:], r[:], r[:])
+            else:
+                nc.scalar.activation(out=r[:], in_=r[:], func=ACT.Square)
+            nc.sync.dma_start(out=out[m : m + MT, t : t + NT], in_=r[:])
 
-        def relu(count):
-            for g in full[:count]:
-                r = outs.tile([MT, NT], F32, name="r")
-                e = EPI[state["n"]]
-                state["n"] += 1
-                if e[0] == "V":
-                    nc.vector.tensor_scalar(out=r[:], in0=acc[g][:], scalar1=0.0, scalar2=None, op0=ALU.max)
-                else:
-                    nc.scalar.activation(out=r[:], in_=acc[g][:], func=ACT.Relu)
-                state["free"] += 1
-                squares.append((g, r, e[1]))
-            del_n = min(count, len(full))
-            full[:] = full[del_n:]
+        HT = NT // 2
 
-        def square():
-            while squares:
-                (m, t), r, e = squares.pop(0)
-                o = outs.tile([MT, NT], F32, name="o")
-                if e == "V":
-                    nc.vector.tensor_mul(o[:], r[:], r[:])
-                else:
-                    nc.scalar.activation(out=o[:], in_=r[:], func=ACT.Square)
-                nc.sync.dma_start(out=out[m : m + MT, t : t + NT], in_=o[:])
+        def multiply_half(m, t, k, h):
+            if k == 0:
+                bank = psum.tile([MT, HT], F32, name="bank")
+                acc[m, t, h] = bank
+            rhs, rhs_scale = xq[t, k]
+            for part, (lhsT, lhsT_scale) in enumerate(wq[m, k]):
+                nc.tensor.matmul_mx(
+                    out=acc[m, t, h][:], lhsT=lhsT, lhsT_scale=lhsT_scale,
+                    rhs=rhs[:, h * HT : (h + 1) * HT], rhs_scale=rhs_scale[:, h * HT : (h + 1) * HT],
+                    start=k == 0 and part == 0, stop=k == PASSES - 1 and part == 1,
+                )
 
-        n = len(units)
-        for s in range(-LEAD, n + 2):
-            if 0 <= s + LEAD < n:
-                first(units[s + LEAD])
-            if 0 <= s + 1 < n:
-                second(units[s + 1])
-            if 0 <= s - 1 < n:
-                quantize(units[s - 1])
-            square()
-            if 0 <= s < n:
-                subtract(units[s])
-            multiply()
-            relu(1 if s <= n else 2)
-        while full or squares:
-            square()
-            relu(2)
-            multiply()
+        def relu_half(m, t, h):
+            r = outs.tile([MT, HT], F32, name="r")
+            relus[m, t, h] = r
+            nc.vector.tensor_scalar(out=r[:], in0=acc[m, t, h][:], scalar1=0.0, scalar2=None, op0=ALU.max)
+
+        def square_half(m, t, h):
+            r = relus[m, t, h]
+            nc.scalar.activation(out=r[:], in_=r[:], func=ACT.Square)
+            nc.sync.dma_start(out=out[m : m + MT, t + h * HT : t + (h + 1) * HT], in_=r[:])
+
+        for op, a, b, c, e in OPS:
+            if op == "pack":
+                pack(a, b, e)
+            elif op == "castS" or op == "castV":
+                cast(a, b, e)
+            elif op == "mask":
+                mask(a, b)
+            elif op == "sub":
+                subtract(a, b)
+            elif op == "qw":
+                quantize(("w", a, b))
+            elif op == "qx":
+                quantize(("x", a, b))
+            elif op == "mm":
+                multiply(a, b, c)
+            elif op == "relu":
+                relu(a, b, e)
+            elif op == "mmh":
+                multiply_half(a, b, c, e)
+            elif op == "reluh":
+                relu_half(a, b, c)
+            elif op == "sqh":
+                square_half(a, b, c)
+            else:
+                square(a, b, e)

@@ -20,208 +20,17 @@ K_PASS = P * PACK
 PASSES = K // K_PASS
 MT = 128
 NT = 512
+HT = NT // 2
 WU = 256
 HI_MASK = 0xFFF0FFF0 - (1 << 32)
-BANKS = 8
-LOADS = [["w",0,512,0],["x",0,512,0],["w",0,512,1],["x",0,512,1],["w",0,512,2],["x",0,512,2],["x",512,512,0],["x",512,512,1],["x",512,512,2],["w",512,256,0],["w",512,256,1],["w",512,256,2],["x",1024,512,0],["x",1024,512,1],["x",1024,512,2],["w",768,256,0],["w",768,256,1],["w",768,256,2]]
-XSHARE = {(512, 2): 0.25, (0, 1): 1, (1024, 0): 0.75, (1024, 2): 1, (512, 1): 0.25, (512, 0): 1, (1024, 1): 0.5, (0, 2): 1, (0, 0): 1}
-OPS = [
-    ["pack",256,0,0,"S"],
-    ["pack",0,0,0,"V"],
-    ["mask",0,0,0,"V"],
-    ["mask",256,0,0,"V"],
-    ["sub",0,0,0,"V"],
-    ["castS",0,0,0,"S"],
-    ["sub",256,0,0,"V"],
-    ["qw",0,0,0,"V"],
-    ["qw",256,0,0,"V"],
-    ["pack",256,1,0,"S"],
-    ["qx",0,0,0,"V"],
-    ["pack",0,1,0,"V"],
-    ["mm",0,0,0,"P"],
-    ["mm",128,0,0,"P"],
-    ["mask",256,1,0,"V"],
-    ["mask",0,1,0,"V"],
-    ["mm",256,0,0,"P"],
-    ["sub",256,1,0,"V"],
-    ["castS",0,1,0,"S"],
-    ["mm",384,0,0,"P"],
-    ["sub",0,1,0,"V"],
-    ["qw",256,1,0,"V"],
-    ["pack",0,2,0,"S"],
-    ["qw",0,1,0,"V"],
-    ["qx",0,1,0,"V"],
-    ["pack",256,2,0,"S"],
-    ["mask",0,2,0,"V"],
-    ["mm",0,0,1,"P"],
-    ["sub",0,2,0,"V"],
-    ["mm",128,0,1,"P"],
-    ["castS",0,2,0,"S"],
-    ["mm",256,0,1,"P"],
-    ["mask",256,2,0,"V"],
-    ["mm",384,0,1,"P"],
-    ["qw",0,2,0,"V"],
-    ["sub",256,2,0,"V"],
-    ["castS",512,0,0,"S"],
-    ["qx",0,2,0,"V"],
-    ["qw",256,2,0,"V"],
-    ["mm",0,0,2,"P"],
-    ["mm",128,0,2,"P"],
-    ["relu",0,0,0,"V"],
-    ["mm",256,0,2,"P"],
-    ["relu",128,0,0,"V"],
-    ["sq",0,0,0,"S"],
-    ["mm",384,0,2,"P"],
-    ["qx",512,0,0,"V"],
-    ["castS",512,1,0,"S"],
-    ["castV",512,1,0,"V"],
-    ["mm",0,512,0,"P"],
-    ["sq",128,0,0,"S"],
-    ["mm",128,512,0,"P"],
-    ["relu",256,0,0,"S"],
-    ["mm",256,512,0,"P"],
-    ["qx",512,1,0,"V"],
-    ["relu",384,0,0,"S"],
-    ["mm",384,512,0,"P"],
-    ["castV",512,2,0,"V"],
-    ["castS",512,2,0,"S"],
-    ["mm",0,512,1,"P"],
-    ["sq",256,0,0,"V"],
-    ["mm",128,512,1,"P"],
-    ["pack",512,0,0,"S"],
-    ["qx",512,2,0,"V"],
-    ["mm",256,512,1,"P"],
-    ["sq",384,0,0,"V"],
-    ["mm",384,512,1,"P"],
-    ["pack",512,1,0,"S"],
-    ["mask",512,0,0,"V"],
-    ["mm",0,512,2,"P"],
-    ["sub",512,0,0,"V"],
-    ["mm",128,512,2,"P"],
-    ["mm",256,512,2,"P"],
-    ["pack",512,2,0,"S"],
-    ["mm",384,512,2,"P"],
-    ["mask",512,1,0,"V"],
-    ["qw",512,0,0,"V"],
-    ["relu",384,512,0,"S"],
-    ["sub",512,1,0,"V"],
-    ["mm",512,0,0,"P"],
-    ["mm",512,512,0,"P"],
-    ["mask",512,2,0,"V"],
-    ["castS",1024,0,0,"S"],
-    ["mm",640,0,0,"P"],
-    ["qw",512,1,0,"V"],
-    ["mm",640,512,0,"P"],
-    ["sub",512,2,0,"V"],
-    ["mm",512,0,1,"P"],
-    ["mm",512,512,1,"P"],
-    ["castV",1024,0,0,"V"],
-    ["mm",640,0,1,"P"],
-    ["qw",512,2,0,"V"],
-    ["castS",1024,1,0,"S"],
-    ["mm",640,512,1,"P"],
-    ["qx",1024,0,0,"V"],
-    ["mm",512,0,2,"P"],
-    ["castV",1024,1,0,"V"],
-    ["mm",512,512,2,"P"],
-    ["relu",512,0,0,"S"],
-    ["relu",0,512,0,"V"],
-    ["mm",640,0,2,"P"],
-    ["relu",512,512,0,"S"],
-    ["qx",1024,1,0,"V"],
-    ["mm",640,512,2,"P"],
-    ["castS",1024,2,0,"S"],
-    ["relu",128,512,0,"V"],
-    ["mm",0,1024,0,"P"],
-    ["relu",256,512,0,"V"],
-    ["mm",0,1024,1,"P"],
-    ["pack",768,0,0,"V"],
-    ["mm",128,1024,0,"P"],
-    ["sq",384,512,0,"V"],
-    ["mm",128,1024,1,"P"],
-    ["sq",0,512,0,"S"],
-    ["qx",1024,2,0,"V"],
-    ["mm",256,1024,0,"P"],
-    ["sq",128,512,0,"S"],
-    ["mm",256,1024,1,"P"],
-    ["mask",768,0,0,"V"],
-    ["sq",256,512,0,"S"],
-    ["pack",768,1,0,"V"],
-    ["mm",0,1024,2,"P"],
-    ["sq",512,512,0,"S"],
-    ["sub",768,0,0,"V"],
-    ["mm",128,1024,2,"P"],
-    ["relu",640,512,0,"S"],
-    ["mm",256,1024,2,"P"],
-    ["relu",128,1024,0,"S"],
-    ["mask",768,1,0,"V"],
-    ["mm",384,1024,0,"P"],
-    ["qw",768,0,0,"V"],
-    ["sq",128,1024,0,"S"],
-    ["mm",384,1024,1,"P"],
-    ["sub",768,1,0,"V"],
-    ["mm",384,1024,2,"P"],
-    ["mm",512,1024,0,"P"],
-    ["pack",768,2,0,"V"],
-    ["mm",512,1024,1,"P"],
-    ["qw",768,1,0,"V"],
-    ["mm",512,1024,2,"P"],
-    ["mask",768,2,0,"V"],
-    ["mm",640,1024,0,"P"],
-    ["sq",512,0,0,"V"],
-    ["mm",640,1024,1,"P"],
-    ["sub",768,2,0,"V"],
-    ["mm",640,1024,2,"P"],
-    ["mm",768,0,0,"P"],
-    ["relu",640,0,0,"V"],
-    ["mm",768,0,1,"P"],
-    ["qw",768,2,0,"V"],
-    ["sq",640,0,0,"S"],
-    ["mm",768,512,0,"P"],
-    ["sq",640,512,0,"V"],
-    ["mm",768,0,2,"P"],
-    ["relu",0,1024,0,"V"],
-    ["mm",768,512,1,"P"],
-    ["relu",768,0,0,"S"],
-    ["relu",256,1024,0,"V"],
-    ["mm",768,512,2,"P"],
-    ["sq",0,1024,0,"S"],
-    ["relu",384,1024,0,"V"],
-    ["mm",768,1024,0,"P"],
-    ["sq",256,1024,0,"S"],
-    ["relu",512,1024,0,"V"],
-    ["mm",768,1024,1,"P"],
-    ["sq",384,1024,0,"V"],
-    ["mm",768,1024,2,"P"],
-    ["sq",512,1024,0,"V"],
-    ["mm",896,0,0,"P"],
-    ["relu",640,1024,0,"V"],
-    ["mm",896,0,1,"P"],
-    ["sq",768,0,0,"V"],
-    ["mm",896,0,2,"P"],
-    ["sq",640,1024,0,"S"],
-    ["relu",768,512,0,"V"],
-    ["mm",896,512,0,"P"],
-    ["relu",768,1024,0,"V"],
-    ["mm",896,512,1,"P"],
-    ["sq",768,512,0,"S"],
-    ["relu",896,0,0,"V"],
-    ["mm",896,512,2,"P"],
-    ["sq",768,1024,0,"S"],
-    ["sq",896,0,0,"S"],
-    ["relu",896,512,0,"V"],
-    ["sq",896,512,0,"S"],
-    ["mmh",896,1024,0,0],
-    ["mmh",896,1024,1,0],
-    ["mmh",896,1024,2,0],
-    ["mmh",896,1024,0,1],
-    ["mmh",896,1024,1,1],
-    ["mmh",896,1024,2,1],
-    ["reluh",896,1024,0,"V"],
-    ["sqh",896,1024,0,"S"],
-    ["reluh",896,1024,1,"V"],
-    ["sqh",896,1024,1,"S"],
+COLUMNS = [("w", 0, 512), ("x", 0, 512), ("x", 512, 512), ("w", 512, 256), ("x", 1024, 512), ("w", 768, 256)]
+LOADS = [
+    [(kind, c0, width, k) for k in range(PASSES) for kind, c0, width in COLUMNS[:2]],
+    *[[(kind, c0, width, k) for k in range(PASSES)] for kind, c0, width in COLUMNS[2:]],
 ]
+VECTOR_PACKS = [(0, 0), (512, 0), (768, 0)]
+SCALAR_SHARE = {0: (1, 1, 1), 512: (1, 0.5, 0.5), 1024: (0.5, 0.5, 0.5)}
+SCALAR_SQUARES = 14
 
 
 def tile_mix_hilo_fm_relu2_kernel(tc, w, x, out):
@@ -231,52 +40,42 @@ def tile_mix_hilo_fm_relu2_kernel(tc, w, x, out):
         stage = ctx.enter_context(tc.tile_pool(name="stage", bufs=4))
         keep = ctx.enter_context(tc.tile_pool(name="keep", bufs=1))
         outs = ctx.enter_context(tc.tile_pool(name="outs", bufs=12))
-        psum = ctx.enter_context(tc.psum_pool(name="psum", bufs=BANKS))
+        psum = ctx.enter_context(tc.psum_pool(name="psum", bufs=8))
         ctx.enter_context(tc.manual_schedule())
 
         warm = keep.tile([P, 1], F32, name="warm")
         nc.vector.memset(warm[:], 0.0)
         nc.scalar.activation(out=warm[:], in_=warm[:], func=ACT.Square)
 
+        steps = [load for part in LOADS for load in part]
         raw_of = {}
-        for kind, c0, width, k in LOADS:
+        raw_bits = {}
+        for kind, c0, width, k in steps:
             raw = raws.tile([P, PACK, width], F32, name="raw_%s%d_%d" % (kind, c0, k))
             src = (w if kind == "w" else x)[k * K_PASS : (k + 1) * K_PASS, c0 : c0 + width]
             nc.sync.dma_start(out=raw[:], in_=src.rearrange("(p j) c -> p j c", j=PACK))
             size = WU if kind == "w" else NT
             for a in range(0, width, size):
-                raw_of[kind, c0 + a, k] = raw[:, :, a : a + size]
+                cols = raw[:, :, a : a + size]
+                raw_of[kind, c0 + a, k] = cols.rearrange("p j (c i) -> p c j i", i=4)
+                if kind == "w":
+                    bits = cols.bitcast(BF16).rearrange("p j (c i h) -> p c j i h", i=4, h=2)
+                    raw_bits[c0 + a, k] = bits[:, :, :, :, 1]
 
         grouped = {}
         wq = {}
         xq = {}
-        acc = {}
-        relus = {}
-        passes = {}
         GR = "p (c i j) -> p c j i"
 
-        def pack(c0, k, e):
+        def pack(c0, k):
             both = stage.tile([P, 2, PACK * WU], BF16, align_bytes=64, name="both")
             grouped["w", c0, k] = both
-            upper = raw_of["w", c0, k].bitcast(BF16).rearrange("p j (c i h) -> p c j i h", i=4, h=2)[:, :, :, :, 1]
             dst = both[:, 0, :].rearrange(GR, i=4, j=PACK)
-            if e == "V":
+            upper = raw_bits[c0, k]
+            if (c0, k) in VECTOR_PACKS:
                 nc.vector.tensor_copy(out=dst, in_=upper)
             else:
                 nc.scalar.copy(out=dst, in_=upper)
-
-        def cast(c0, k, e):
-            u = ("x", c0, k)
-            if u not in grouped:
-                grp = stage.tile([P, PACK * NT], BF16, align_bytes=64, name="grp")
-                grouped[u] = grp
-            cut = int(XSHARE.get((c0, k), 1.0) * NT) // 4
-            src = raw_of[u].rearrange("p j (c i) -> p c j i", i=4)
-            dst = grouped[u][:].rearrange(GR, i=4, j=PACK)
-            if e == "S":
-                nc.scalar.copy(out=dst[:, :cut], in_=src[:, :cut])
-            else:
-                nc.vector.tensor_copy(out=dst[:, cut:], in_=src[:, cut:])
 
         def mask(c0, k):
             hi = grouped["w", c0, k][:, 0, :].bitcast(I32)
@@ -286,17 +85,26 @@ def tile_mix_hilo_fm_relu2_kernel(tc, w, x, out):
             both = grouped["w", c0, k]
             nc.vector.tensor_tensor(
                 out=both[:, 1, :].rearrange(GR, i=4, j=PACK),
-                in0=raw_of["w", c0, k].rearrange("p j (c i) -> p c j i", i=4),
+                in0=raw_of["w", c0, k],
                 in1=both[:, 0, :].rearrange(GR, i=4, j=PACK),
                 op=ALU.subtract,
             )
 
-        def quantize(u):
-            kind, c0, k = u
+        def cast(c0, k):
+            grp = stage.tile([P, PACK * NT], BF16, align_bytes=64, name="grp")
+            grouped["x", c0, k] = grp
+            cut = int(SCALAR_SHARE[c0][k] * NT) // 4
+            src = raw_of["x", c0, k]
+            dst = grp[:].rearrange(GR, i=4, j=PACK)
+            nc.scalar.copy(out=dst[:, :cut], in_=src[:, :cut])
+            if cut < NT // 4:
+                nc.vector.tensor_copy(out=dst[:, cut:], in_=src[:, cut:])
+
+        def quantize(kind, c0, k):
             width = 2 * WU if kind == "w" else NT
-            codes = keep.tile([P, width], U32, align_bytes=256, name="codes_%s%d_%d" % u)
-            scales = keep.tile([P, width], U8, align_bytes=256, name="scales_%s%d_%d" % u)
-            src = grouped.pop(u)
+            codes = keep.tile([P, width], U32, align_bytes=256, name="codes_%s%d_%d" % (kind, c0, k))
+            scales = keep.tile([P, width], U8, align_bytes=256, name="scales_%s%d_%d" % (kind, c0, k))
+            src = grouped.pop((kind, c0, k))
             nc.vector.quantize_mx(
                 out=codes[:].bitcast(FP8X4),
                 scales=scales[:],
@@ -308,83 +116,109 @@ def tile_mix_hilo_fm_relu2_kernel(tc, w, x, out):
                         (codes[:, b : b + MT].bitcast(FP8X4), scales[:, b : b + MT]) for b in (a, WU + a)
                     ]
             else:
-                xq[c0, k] = (codes[:].bitcast(FP8X4), scales[:])
+                xq[c0, k] = (codes[:], scales)
 
-        def multiply(m, t, k):
-            n = passes.get((m, t), 0)
-            if n == 0:
-                bank = psum.tile([MT, NT], F32, name="bank")
-                acc[m, t] = bank
-            rhs, rhs_scale = xq[t, k]
-            for h, (lhsT, lhsT_scale) in enumerate(wq[m, k]):
-                nc.tensor.matmul_mx(
-                    out=acc[m, t][:], lhsT=lhsT, lhsT_scale=lhsT_scale, rhs=rhs, rhs_scale=rhs_scale,
-                    start=n == 0 and h == 0, stop=n == PASSES - 1 and h == 1,
-                )
-            passes[m, t] = n + 1
+        def blocks(m0, m1, ts):
+            return [(m, t) for m in range(m0, m1, MT) for t in ts]
 
-        def relu(m, t, e):
-            r = outs.tile([MT, NT], F32, name="r")
-            relus[m, t] = r
-            if e == "V":
-                nc.vector.tensor_scalar(out=r[:], in0=acc[m, t][:], scalar1=0.0, scalar2=None, op0=ALU.max)
+        batches = [
+            blocks(0, 512, (0,)),
+            blocks(0, 512, (512,)),
+            blocks(512, 768, (0, 512)),
+            blocks(0, 768, (1024,)),
+            blocks(768, 1024, (0, 512, 1024)),
+        ]
+        order = [block for batch in batches for block in batch]
+        tiles = [(m, t, NT) for m, t in order[:-1]] + [(order[-1][0], order[-1][1] + a, HT) for a in (0, HT)]
+        passes = []
+        n = 0
+        for batch in batches:
+            size = len(batch)
+            here = range(n, n + size) if n + size < len(order) else range(n, len(tiles))
+            n += size
+            if n <= 12:
+                passes += [(b, k) for k in range(PASSES) for b in here]
             else:
-                nc.scalar.activation(out=r[:], in_=acc[m, t][:], func=ACT.Relu)
+                passes += [(b, k) for b in here for k in range(PASSES)]
 
-        def square(m, t, e):
-            r = relus[m, t]
-            if e == "V":
-                nc.vector.tensor_mul(r[:], r[:], r[:])
-            else:
+        acc = {}
+        relus = {}
+
+        def multiply():
+            while passes:
+                b, k = passes[0]
+                m, t, width = tiles[b]
+                t0 = t // NT * NT
+                if (m, k) not in wq or (t0, k) not in xq:
+                    return
+                passes.pop(0)
+                if k == 0:
+                    bank = psum.tile([MT, width], F32, name="bank")
+                    acc[b] = bank
+                codes, scales = xq[t0, k]
+                cols = slice(t - t0, t - t0 + width)
+                for part, (lhsT, lhsT_scale) in enumerate(wq[m, k]):
+                    nc.tensor.matmul_mx(
+                        out=acc[b][:],
+                        lhsT=lhsT,
+                        lhsT_scale=lhsT_scale,
+                        rhs=codes[:, cols].bitcast(FP8X4),
+                        rhs_scale=scales[:, cols],
+                        start=k == 0 and part == 0,
+                        stop=k == PASSES - 1 and part == 1,
+                    )
+
+        def relu(b):
+            r = outs.tile([MT, tiles[b][2]], F32, name="r")
+            relus[b] = r
+            nc.scalar.activation(out=r[:], in_=acc[b][:], func=ACT.Relu)
+
+        def square(b):
+            m, t, width = tiles[b]
+            r = relus[b]
+            if b < SCALAR_SQUARES:
                 nc.scalar.activation(out=r[:], in_=r[:], func=ACT.Square)
-            nc.sync.dma_start(out=out[m : m + MT, t : t + NT], in_=r[:])
-
-        HT = NT // 2
-
-        def multiply_half(m, t, k, h):
-            if k == 0:
-                bank = psum.tile([MT, HT], F32, name="bank")
-                acc[m, t, h] = bank
-            rhs, rhs_scale = xq[t, k]
-            for part, (lhsT, lhsT_scale) in enumerate(wq[m, k]):
-                nc.tensor.matmul_mx(
-                    out=acc[m, t, h][:], lhsT=lhsT, lhsT_scale=lhsT_scale,
-                    rhs=rhs[:, h * HT : (h + 1) * HT], rhs_scale=rhs_scale[:, h * HT : (h + 1) * HT],
-                    start=k == 0 and part == 0, stop=k == PASSES - 1 and part == 1,
-                )
-
-        def relu_half(m, t, h):
-            r = outs.tile([MT, HT], F32, name="r")
-            relus[m, t, h] = r
-            nc.vector.tensor_scalar(out=r[:], in0=acc[m, t, h][:], scalar1=0.0, scalar2=None, op0=ALU.max)
-
-        def square_half(m, t, h):
-            r = relus[m, t, h]
-            nc.scalar.activation(out=r[:], in_=r[:], func=ACT.Square)
-            nc.sync.dma_start(out=out[m : m + MT, t + h * HT : t + (h + 1) * HT], in_=r[:])
-
-        for op, a, b, c, e in OPS:
-            if op == "pack":
-                pack(a, b, e)
-            elif op == "castS" or op == "castV":
-                cast(a, b, e)
-            elif op == "mask":
-                mask(a, b)
-            elif op == "sub":
-                subtract(a, b)
-            elif op == "qw":
-                quantize(("w", a, b))
-            elif op == "qx":
-                quantize(("x", a, b))
-            elif op == "mm":
-                multiply(a, b, c)
-            elif op == "relu":
-                relu(a, b, e)
-            elif op == "mmh":
-                multiply_half(a, b, c, e)
-            elif op == "reluh":
-                relu_half(a, b, c)
-            elif op == "sqh":
-                square_half(a, b, c)
             else:
-                square(a, b, e)
+                nc.vector.tensor_mul(r[:], r[:], r[:])
+            nc.sync.dma_start(out=out[m : m + MT, t : t + width], in_=r[:])
+
+        slots = {}
+        for b in range(len(tiles)):
+            s = 9 + 9 * b // 10
+            slots.setdefault(s, []).append((b, relu))
+            slots.setdefault(s + 2, []).append((b, square))
+
+        waiting = []
+        for i in range(max(slots) + 1):
+            if i < len(steps):
+                kind, c0, width, k = steps[i]
+                if kind == "x":
+                    cast(c0, k)
+                    for c in waiting:
+                        quantize("w", *c)
+                    waiting = []
+                    quantize("x", c0, k)
+                elif width > WU:
+                    halves = range(c0, c0 + width, WU)
+                    for c in halves:
+                        pack(c, k)
+                    for c in halves:
+                        mask(c, k)
+                    for c in halves:
+                        subtract(c, k)
+                    for c in halves:
+                        quantize("w", c, k)
+                else:
+                    pack(c0, k)
+                    mask(c0, k)
+                    for c in waiting:
+                        quantize("w", *c)
+                    subtract(c0, k)
+                    waiting = [(c0, k)]
+            else:
+                for c in waiting:
+                    quantize("w", *c)
+                waiting = []
+            multiply()
+            for b, act in sorted(slots.get(i, []), key=lambda item: item[0]):
+                act(b)

from contextlib import ExitStack

import concourse.mybir as mybir

K, M, T = 1536, 1024, 1536
FLOPS = 2 * 2 * K * M * T

F32 = mybir.dt.float32
BF16 = mybir.dt.bfloat16
U32 = mybir.dt.uint32
I32 = mybir.dt.int32
U8 = mybir.dt.uint8
FP8X4 = mybir.dt.float8_e4m3fn_x4
ALU = mybir.AluOpType
ACT = mybir.ActivationFunctionType

P = 128
PACK = 4
K_PASS = P * PACK
PASSES = K // K_PASS
MT = 128
NT = 512
HT = NT // 2
WU = 256
HI_MASK = 0xFFF0FFF0 - (1 << 32)
COLUMNS = [("w", 0, 512), ("x", 0, 512), ("x", 512, 512), ("w", 512, 256), ("x", 1024, 512), ("w", 768, 256)]
LOADS = [
    [(kind, c0, width, k) for k in range(PASSES) for kind, c0, width in COLUMNS[:2]],
    *[[(kind, c0, width, k) for k in range(PASSES)] for kind, c0, width in COLUMNS[2:]],
]
VECTOR_PACKS = [(0, 0), (512, 0), (768, 0)]
SCALAR_SHARE = {0: (1, 1, 1), 512: (1, 0.5, 0.5), 1024: (0.5, 0.5, 0.5)}
SCALAR_SQUARES = 14


def tile_mix_hilo_fm_relu2_kernel(tc, w, x, out):
    nc = tc.nc
    with ExitStack() as ctx:
        raws = ctx.enter_context(tc.tile_pool(name="raws", bufs=1))
        stage = ctx.enter_context(tc.tile_pool(name="stage", bufs=4))
        keep = ctx.enter_context(tc.tile_pool(name="keep", bufs=1))
        outs = ctx.enter_context(tc.tile_pool(name="outs", bufs=12))
        psum = ctx.enter_context(tc.psum_pool(name="psum", bufs=8))
        ctx.enter_context(tc.manual_schedule())

        warm = keep.tile([P, 1], F32, name="warm")
        nc.vector.memset(warm[:], 0.0)
        nc.scalar.activation(out=warm[:], in_=warm[:], func=ACT.Square)

        steps = [load for part in LOADS for load in part]
        raw_of = {}
        raw_bits = {}
        for kind, c0, width, k in steps:
            raw = raws.tile([P, PACK, width], F32, name="raw_%s%d_%d" % (kind, c0, k))
            src = (w if kind == "w" else x)[k * K_PASS : (k + 1) * K_PASS, c0 : c0 + width]
            nc.sync.dma_start(out=raw[:], in_=src.rearrange("(p j) c -> p j c", j=PACK))
            size = WU if kind == "w" else NT
            for a in range(0, width, size):
                cols = raw[:, :, a : a + size]
                raw_of[kind, c0 + a, k] = cols.rearrange("p j (c i) -> p c j i", i=4)
                if kind == "w":
                    bits = cols.bitcast(BF16).rearrange("p j (c i h) -> p c j i h", i=4, h=2)
                    raw_bits[c0 + a, k] = bits[:, :, :, :, 1]

        grouped = {}
        wq = {}
        xq = {}
        GR = "p (c i j) -> p c j i"

        def pack(c0, k):
            both = stage.tile([P, 2, PACK * WU], BF16, align_bytes=64, name="both")
            grouped["w", c0, k] = both
            dst = both[:, 0, :].rearrange(GR, i=4, j=PACK)
            upper = raw_bits[c0, k]
            if (c0, k) in VECTOR_PACKS:
                nc.vector.tensor_copy(out=dst, in_=upper)
            else:
                nc.scalar.copy(out=dst, in_=upper)

        def mask(c0, k):
            hi = grouped["w", c0, k][:, 0, :].bitcast(I32)
            nc.vector.tensor_scalar(out=hi, in0=hi, scalar1=HI_MASK, scalar2=None, op0=ALU.bitwise_and)

        def subtract(c0, k):
            both = grouped["w", c0, k]
            nc.vector.tensor_tensor(
                out=both[:, 1, :].rearrange(GR, i=4, j=PACK),
                in0=raw_of["w", c0, k],
                in1=both[:, 0, :].rearrange(GR, i=4, j=PACK),
                op=ALU.subtract,
            )

        def cast(c0, k):
            grp = stage.tile([P, PACK * NT], BF16, align_bytes=64, name="grp")
            grouped["x", c0, k] = grp
            cut = int(SCALAR_SHARE[c0][k] * NT) // 4
            src = raw_of["x", c0, k]
            dst = grp[:].rearrange(GR, i=4, j=PACK)
            nc.scalar.copy(out=dst[:, :cut], in_=src[:, :cut])
            if cut < NT // 4:
                nc.vector.tensor_copy(out=dst[:, cut:], in_=src[:, cut:])

        def quantize(kind, c0, k):
            width = 2 * WU if kind == "w" else NT
            codes = keep.tile([P, width], U32, align_bytes=256, name="codes_%s%d_%d" % (kind, c0, k))
            scales = keep.tile([P, width], U8, align_bytes=256, name="scales_%s%d_%d" % (kind, c0, k))
            src = grouped.pop((kind, c0, k))
            nc.vector.quantize_mx(
                out=codes[:].bitcast(FP8X4),
                scales=scales[:],
                in_=src[:].rearrange("p h c -> p (h c)") if kind == "w" else src[:],
            )
            if kind == "w":
                for a in range(0, WU, MT):
                    wq[c0 + a, k] = [
                        (codes[:, b : b + MT].bitcast(FP8X4), scales[:, b : b + MT]) for b in (a, WU + a)
                    ]
            else:
                xq[c0, k] = (codes[:], scales)

        def blocks(m0, m1, ts):
            return [(m, t) for m in range(m0, m1, MT) for t in ts]

        batches = [
            blocks(0, 512, (0,)),
            blocks(0, 512, (512,)),
            blocks(512, 768, (0, 512)),
            blocks(0, 768, (1024,)),
            blocks(768, 1024, (0, 512, 1024)),
        ]
        order = [block for batch in batches for block in batch]
        tiles = [(m, t, NT) for m, t in order[:-1]] + [(order[-1][0], order[-1][1] + a, HT) for a in (0, HT)]
        passes = []
        n = 0
        for batch in batches:
            size = len(batch)
            here = range(n, n + size) if n + size < len(order) else range(n, len(tiles))
            n += size
            if n <= 12:
                passes += [(b, k) for k in range(PASSES) for b in here]
            else:
                passes += [(b, k) for b in here for k in range(PASSES)]

        acc = {}
        relus = {}

        def multiply():
            while passes:
                b, k = passes[0]
                m, t, width = tiles[b]
                t0 = t // NT * NT
                if (m, k) not in wq or (t0, k) not in xq:
                    return
                passes.pop(0)
                if k == 0:
                    bank = psum.tile([MT, width], F32, name="bank")
                    acc[b] = bank
                codes, scales = xq[t0, k]
                cols = slice(t - t0, t - t0 + width)
                for part, (lhsT, lhsT_scale) in enumerate(wq[m, k]):
                    nc.tensor.matmul_mx(
                        out=acc[b][:],
                        lhsT=lhsT,
                        lhsT_scale=lhsT_scale,
                        rhs=codes[:, cols].bitcast(FP8X4),
                        rhs_scale=scales[:, cols],
                        start=k == 0 and part == 0,
                        stop=k == PASSES - 1 and part == 1,
                    )

        def relu(b):
            r = outs.tile([MT, tiles[b][2]], F32, name="r")
            relus[b] = r
            nc.scalar.activation(out=r[:], in_=acc[b][:], func=ACT.Relu)

        def square(b):
            m, t, width = tiles[b]
            r = relus[b]
            if b < SCALAR_SQUARES:
                nc.scalar.activation(out=r[:], in_=r[:], func=ACT.Square)
            else:
                nc.vector.tensor_mul(r[:], r[:], r[:])
            nc.sync.dma_start(out=out[m : m + MT, t : t + width], in_=r[:])

        slots = {}
        for b in range(len(tiles)):
            s = 9 + 9 * b // 10
            slots.setdefault(s, []).append((b, relu))
            slots.setdefault(s + 2, []).append((b, square))

        waiting = []
        for i in range(max(slots) + 1):
            if i < len(steps):
                kind, c0, width, k = steps[i]
                if kind == "x":
                    cast(c0, k)
                    for c in waiting:
                        quantize("w", *c)
                    waiting = []
                    quantize("x", c0, k)
                elif width > WU:
                    halves = range(c0, c0 + width, WU)
                    for c in halves:
                        pack(c, k)
                    for c in halves:
                        mask(c, k)
                    for c in halves:
                        subtract(c, k)
                    for c in halves:
                        quantize("w", c, k)
                else:
                    pack(c0, k)
                    mask(c0, k)
                    for c in waiting:
                        quantize("w", *c)
                    subtract(c0, k)
                    waiting = [(c0, k)]
            else:
                for c in waiting:
                    quantize("w", *c)
                waiting = []
            multiply()
            for b, act in sorted(slots.get(i, []), key=lambda item: item[0]):
                act(b)
